import numpy as np
import ml_dtypes


def mxq(x, axis, fmt="e4m3"):
    dtype, down = {"e4m3": (ml_dtypes.float8_e4m3fn, 7), "e5m2": (ml_dtypes.float8_e5m2, 14)}[fmt]
    v = np.moveaxis(np.asarray(x, np.float32).astype(ml_dtypes.bfloat16).astype(np.float64), axis, -1)
    blocks = v.reshape(v.shape[:-1] + (-1, 32))
    amax = np.abs(blocks).max(-1, keepdims=True)
    byte = np.maximum(np.where(amax > 0, np.frexp(amax)[1] - 1 + 127, 0) - down, 1)
    scale = np.exp2(byte - 127.0)
    codes = (blocks / scale).astype(np.float32).astype(dtype).astype(np.float64)
    return np.moveaxis((codes * scale).reshape(v.shape), -1, axis)


WIDE = False


def mx_kscale(k):
    if not WIDE:
        return np.ones(k)
    levels = np.array([10, -10, 5, -5, 0])
    if k % 512:
        return np.exp2(np.random.permutation(np.resize(levels, k // 32))).repeat(32)
    a = np.empty((k // 512, 16))
    for p in range(k // 512):
        a[p, :8] = np.random.permutation(np.resize(levels, 8))
        for g in range(8):
            far = levels[np.abs(levels - a[p, g]) >= 10]
            a[p, g + 8] = far[np.random.randint(len(far))]
    return np.exp2(a.ravel()).repeat(32)


def f64(x):
    return np.asarray(x).astype(np.float64)


def striped(idx):
    return np.tile(idx.reshape(-1, 16).T, (8, 1)).astype(np.uint16)


def unstriped(offs):
    return offs[:16].T.reshape(-1).astype(np.int64)


def d_relu(v):
    return (v > 0).astype(np.float64)


K, T, E, C, H, N = 256, 1024, 8, 256, 512, 512


def by_expert(wq, xq):
    return np.concatenate([wq[e].T @ xq[:, e * C:(e + 1) * C] for e in range(E)], axis=1)


def setup_inputs():
    n = np.random.standard_normal
    s = mx_kscale(N)[:, None]
    u = mx_kscale(H)
    first = np.random.permutation(np.repeat(np.arange(E), T // E))
    second = (first + 1 + np.random.permutation(np.repeat(np.arange(E - 1), -(-T // (E - 1)))[:T])) % E
    while np.bincount(second, minlength=E).max() != T // E:
        load = np.bincount(second, minlength=E); hi, lo = int(load.argmax()), int(load.argmin())
        t = np.flatnonzero((second == hi) & (first != lo))[0]; second[t] = lo
    slot_token = np.empty(E * C, np.int64); pos = np.empty((2, T), np.int64); fill = np.zeros(E, np.int64)
    place = np.stack([np.random.permutation(C) for _ in range(E)])
    for r, deal in enumerate((first, second)):
        for t in np.random.permutation(T):
            e = deal[t]; j = e * C + place[e, fill[e]]; fill[e] += 1; slot_token[j] = t; pos[r, t] = j
    g = np.random.uniform(0.2, 0.8, T)
    w_slot = np.empty(E * C); w_slot[pos[0]] = g; w_slot[pos[1]] = 1.0 - g
    return {
        "dyT": (n((N, T)) * s).astype(np.float32),
        "a": n((H, E * C)).astype(np.float32),
        "w2": (n((E, N, H)) / np.sqrt(N) / s[None] * u[None, None, :]).astype(np.float32),
        "w1": (n((E, H, K)) / np.sqrt(H) / u[None, :, None]).astype(np.float32),
        "gate": np.tile(w_slot, (N, 1)).astype(np.float32),
        "offs": striped(slot_token),
        "pos1": striped(pos[0]),
        "pos2": striped(pos[1]),
    }


def reference(dyT, a, w2, w1, gate, offs, pos1, pos2):
    idx = unstriped(offs)
    gq = mxq(f64(gate) * f64(dyT)[:, idx], 0, "e4m3")
    dh = by_expert(mxq(f64(w2), 1, "e4m3"), gq)
    da = dh * d_relu(f64(a))
    dx = by_expert(mxq(f64(w1), 1, "e4m3"), mxq(da, 0, "e4m3"))
    return dx[:, unstriped(pos1)] + dx[:, unstriped(pos2)]

@@ -1,0 +1,255 @@
+from contextlib import ExitStack
+
+import concourse.mybir as mybir
+
+K, T, E, C, H, N = 256, 1024, 8, 256, 512, 512
+S = E * C
+FLOPS = 2 * S * N * H + 2 * S * H * K
+BYTES = 4 * (N * T + H * S + E * N * H + E * H * K + S + K * T) + 2 * 128 * (S + 2 * T) // 16
+
+F32 = mybir.dt.float32
+BF16 = mybir.dt.bfloat16
+U32 = mybir.dt.uint32
+U16 = mybir.dt.uint16
+U8 = mybir.dt.uint8
+FP8X4 = mybir.dt.float8_e4m3fn_x4
+ALU = mybir.AluOpType
+
+P = 128
+PACK = 4
+PAIR = 2 * C
+PAIRS = E // 2
+CHUNK = 128
+EARLY = 4
+
+
+def tile_moe_bdx_mlp_relu_kernel(tc, dyT, a, w2, w1, gate, offs, pos1, pos2, out):
+    nc = tc.nc
+    with ExitStack() as ctx:
+        held = ctx.enter_context(tc.tile_pool(name="held", bufs=1))
+        raw = ctx.enter_context(tc.tile_pool(name="raw", bufs=4))
+        mid = ctx.enter_context(tc.tile_pool(name="mid", bufs=3))
+        psum = ctx.enter_context(tc.psum_pool(name="psum", bufs=5))
+
+        offs_sb = held.tile([P, S // 16], U16, name="offs_sb")
+        pos1_sb = held.tile([P, T // 16], U16, name="pos1_sb")
+        pos2_sb = held.tile([P, T // 16], U16, name="pos2_sb")
+        dy = [held.tile([P, T], F32, name=f"dy{t}") for t in range(PACK)]
+        gates = [held.tile([P, PAIR], F32, name=f"gate{q}") for q in range(PAIRS)]
+        dx = [held.tile([P, S], F32, name=f"dx{h}") for h in range(2)]
+
+        dy_view = dyT.rearrange("(p t) m -> p t m", t=PACK)
+        a_view = a.rearrange("(p t) m -> p t m", t=PACK)
+
+        w2_raw, w1_raw, a_raw = {}, {}, {}
+
+        def load_dy(t):
+            nc.sync.dma_start(out=dy[t][:], in_=dy_view[:, t, :])
+
+        def load_gate(q):
+            nc.sync.dma_start(out=gates[q][:], in_=gate[0:P, q * PAIR : (q + 1) * PAIR])
+
+        def load_w2(e, halves=(0, 1)):
+            w2_raw.setdefault(e, {})
+            src = w2[e].rearrange("(p j) c -> p j c", j=PACK)
+            for i in halves:
+                w2_raw[e][i] = raw.tile([P, PACK, H // 2], F32, name="w2_raw", bufs=7)
+                nc.sync.dma_start(out=w2_raw[e][i][:], in_=src[:, :, i * (H // 2) : (i + 1) * (H // 2)])
+
+        def load_w1(e):
+            w1_raw[e] = raw.tile([P, PACK, K], F32, name="w1_raw", bufs=6)
+            nc.sync.dma_start(out=w1_raw[e][:], in_=w1[e].rearrange("(p j) c -> p j c", j=PACK))
+
+        def load_a(q):
+            a_raw[q] = raw.tile([P, PACK, PAIR], F32, name="a_raw", bufs=3)
+            nc.sync.dma_start(out=a_raw[q][:], in_=a_view[:, :, q * PAIR : (q + 1) * PAIR])
+
+        w2_q, w1_bf, w1_q, g_q, da_q, g4 = {}, {}, {}, {}, {}, {}
+
+        def gather(q):
+            g4[q] = mid.tile([P, PACK, PAIR], F32, name="g4", bufs=4)
+            for t in range(PACK):
+                nc.vector.tensor_tensor(
+                    g4[q][:, t, :],
+                    dy[t][:].indirect(offs_sb[:, q * (PAIR // 16) : (q + 1) * (PAIR // 16)]),
+                    gates[q][:],
+                    ALU.mult,
+                )
+
+        def quantize(dst, lo, hi, src):
+            nc.vector.quantize_mx(out=dst[0][:, lo:hi].bitcast(FP8X4), scales=dst[1][:, lo:hi], in_=src)
+
+        def make_g(q):
+            g_bf = mid.tile([P, PAIR * PACK], BF16, name="g_bf", bufs=2, align_bytes=64)
+            nc.scalar.copy(
+                g_bf[:].rearrange("p (c i t) -> p c t i", i=4, t=PACK),
+                g4[q][:].rearrange("p t (c i) -> p c t i", i=4),
+            )
+            g_q[q] = (
+                mid.tile([P, PAIR], U32, name="g_codes", bufs=2, align_bytes=64),
+                mid.tile([P, PAIR], U8, name="g_scales", bufs=2, align_bytes=64),
+            )
+            quantize(g_q[q], 0, PAIR, g_bf[:])
+
+        def make_w2(e):
+            w2_bf = mid.tile([P, H * PACK], BF16, name="w2_bf", bufs=3, align_bytes=64)
+            dst = w2_bf[:].rearrange("p (t m j) -> p m j t", t=PACK, j=PACK)
+            for i in range(2):
+                nc.scalar.copy(
+                    dst[:, i * 64 : (i + 1) * 64],
+                    w2_raw[e][i][:].rearrange("p j (m t) -> p m j t", t=PACK),
+                )
+            w2_q[e] = (
+                mid.tile([P, H], U32, name="w2_codes", bufs=5, align_bytes=64),
+                mid.tile([P, H], U8, name="w2_scales", bufs=5, align_bytes=64),
+            )
+            quantize(w2_q[e], 0, H, w2_bf[:])
+
+        def cast_w1(e, h0, h1):
+            if e not in w1_bf:
+                w1_bf[e] = mid.tile([P, K * PACK], BF16, name="w1_bf", bufs=5, align_bytes=64)
+                w1_q[e] = (
+                    mid.tile([P, K], U32, name="w1_codes", bufs=6, align_bytes=64),
+                    mid.tile([P, K], U8, name="w1_scales", bufs=6, align_bytes=64),
+                )
+            lo, hi = h0 * 128, h1 * 128
+            nc.scalar.copy(
+                w1_bf[e][:, lo * PACK : hi * PACK].rearrange("p (c i t) -> p c t i", i=4, t=PACK),
+                w1_raw[e][:, :, lo:hi].rearrange("p t (c i) -> p c t i", i=4),
+            )
+
+        def quantize_w1(e, h0, h1):
+            lo, hi = h0 * 128, h1 * 128
+            quantize(w1_q[e], lo, hi, w1_bf[e][:, lo * PACK : hi * PACK])
+
+        def stage1(e):
+            q, base = e // 2, (e % 2) * C
+            da_bf = mid.tile([P, C * PACK], BF16, name="da_bf", bufs=3, align_bytes=64)
+            for c in range(C // CHUNK):
+                lo = base + c * CHUNK
+                bank = psum.tile([P, PACK, CHUNK], F32, name="bank1", bufs=5)
+                for t in range(PACK):
+                    nc.tensor.matmul_mx(
+                        out=bank[:, t, :],
+                        lhsT=w2_q[e][0][:, t * P : (t + 1) * P].bitcast(FP8X4),
+                        lhsT_scale=w2_q[e][1][:, t * P : (t + 1) * P],
+                        rhs=g_q[q][0][:, lo : lo + CHUNK].bitcast(FP8X4),
+                        rhs_scale=g_q[q][1][:, lo : lo + CHUNK],
+                        start=True,
+                        stop=True,
+                    )
+                nc.vector.scalar_tensor_tensor(
+                    out=da_bf[:, c * CHUNK * PACK : (c + 1) * CHUNK * PACK].rearrange("p (m t) -> p m t", t=PACK),
+                    in0=a_raw[q][:, :, lo : lo + CHUNK].rearrange("p t m -> p m t"),
+                    scalar=0.0,
+                    in1=bank[:].rearrange("p t m -> p m t"),
+                    op0=ALU.is_gt,
+                    op1=ALU.mult,
+                )
+            da_q[e] = (
+                mid.tile([P, C], U32, name="da_codes", bufs=6, align_bytes=64),
+                mid.tile([P, C], U8, name="da_scales", bufs=6, align_bytes=64),
+            )
+            quantize(da_q[e], 0, C, da_bf[:])
+
+        def stage2(q, h):
+            bank = psum.tile([P, PAIR], F32, name="bank2", bufs=3)
+            for i in range(2):
+                e = 2 * q + i
+                nc.tensor.matmul_mx(
+                    out=bank[:, i * C : (i + 1) * C],
+                    lhsT=w1_q[e][0][:, h * P : (h + 1) * P].bitcast(FP8X4),
+                    lhsT_scale=w1_q[e][1][:, h * P : (h + 1) * P],
+                    rhs=da_q[e][0][:].bitcast(FP8X4),
+                    rhs_scale=da_q[e][1][:],
+                    start=True,
+                    stop=True,
+                )
+            nc.scalar.copy(dx[h][:, q * PAIR : (q + 1) * PAIR], bank[:])
+
+        picked = {}
+
+        def pick(h, which, lo, hi):
+            if (h, which) not in picked:
+                picked[h, which] = mid.tile([P, T], F32, name=f"pick{which}", bufs=2)
+            pos = (pos1_sb, pos2_sb)[which]
+            nc.vector.tensor_copy(picked[h, which][:, lo:hi], dx[h][:].indirect(pos[:, lo // 16 : hi // 16]))
+
+        def combine(h, lo, hi, engine):
+            o = picked[h, 0][:, lo:hi]
+            engine.tensor_tensor(o, o, picked[h, 1][:, lo:hi], ALU.add)
+            nc.sync.dma_start(out=out[h * P : (h + 1) * P, lo:hi], in_=o)
+
+        nc.sync.dma_start(offs_sb[:], offs)
+        load_dy(0)
+        load_gate(0)
+        load_w2(0, (0,))
+        load_gate(1)
+        load_w2(0, (1,))
+        load_gate(2)
+        load_w2(1, (0,))
+        load_gate(3)
+        load_w2(1, (1,))
+        load_dy(1)
+        load_w2(2)
+        load_dy(2)
+        load_w2(3, (0,))
+        load_dy(3)
+        load_w1(0)
+        load_w2(3, (1,))
+        load_a(0)
+        load_w1(1)
+        nc.sync.dma_start(pos1_sb[:], pos1)
+        nc.sync.dma_start(pos2_sb[:], pos2)
+
+        make_w2(0)
+        make_w2(1)
+        make_w2(2)
+        gather(0)
+        gather(1)
+        make_g(0)
+        make_w2(3)
+        load_a(1)
+        load_w1(2)
+        load_w1(3)
+        for q in range(PAIRS):
+            for e in (2 * q, 2 * q + 1):
+                if e + 4 < E:
+                    load_w2(e + 4)
+            if q + 2 < PAIRS:
+                load_w1(2 * q + 4)
+                load_a(q + 2)
+                load_w1(2 * q + 5)
+            for e in (2 * q, 2 * q + 1):
+                stage1(e)
+            if q + 2 < PAIRS:
+                gather(q + 2)
+            if q + 1 < PAIRS:
+                make_g(q + 1)
+            for e in (2 * q, 2 * q + 1):
+                hh = 2 if e < EARLY else 1
+                cast_w1(e, 0, hh)
+                quantize_w1(e, 0, hh)
+                if e + 4 < E:
+                    make_w2(e + 4)
+            stage2(q, 0)
+            if 2 * q < EARLY:
+                stage2(q, 1)
+        for e in range(EARLY, E):
+            cast_w1(e, 1, 2)
+        pick(0, 0, 0, T)
+        for e in range(EARLY, E):
+            quantize_w1(e, 1, 2)
+        for q in range(EARLY // 2, PAIRS):
+            stage2(q, 1)
+        pick(0, 1, 0, T // 2)
+        combine(0, 0, T // 2, nc.gpsimd)
+        pick(0, 1, T // 2, T)
+        combine(0, T // 2, T, nc.gpsimd)
+        pick(1, 0, 0, T)
+        pick(1, 1, 0, T // 2)
+        combine(1, 0, T // 2, nc.gpsimd)
+        pick(1, 1, T // 2, 3 * T // 4)
+        pick(1, 1, 3 * T // 4, T)
+        combine(1, T // 2, 3 * T // 4, nc.vector)
+        combine(1, 3 * T // 4, T, nc.vector)

@@ -20,7 +20,7 @@ PACK = 4
 PAIR = 2 * C
 PAIRS = E // 2
 CHUNK = 128
-EARLY = 4
+EARLY = 2
 
 
 def tile_moe_bdx_mlp_relu_kernel(tc, dyT, a, w2, w1, gate, offs, pos1, pos2, out):
@@ -49,12 +49,9 @@ def tile_moe_bdx_mlp_relu_kernel(tc, dyT, a, w2, w1, gate, offs, pos1, pos2, out
         def load_gate(q):
             nc.sync.dma_start(out=gates[q][:], in_=gate[0:P, q * PAIR : (q + 1) * PAIR])
 
-        def load_w2(e, halves=(0, 1)):
-            w2_raw.setdefault(e, {})
-            src = w2[e].rearrange("(p j) c -> p j c", j=PACK)
-            for i in halves:
-                w2_raw[e][i] = raw.tile([P, PACK, H // 2], F32, name="w2_raw", bufs=7)
-                nc.sync.dma_start(out=w2_raw[e][i][:], in_=src[:, :, i * (H // 2) : (i + 1) * (H // 2)])
+        def load_w2(e):
+            w2_raw[e] = raw.tile([P, PACK, H], F32, name="w2_raw", bufs=4)
+            nc.sync.dma_start(out=w2_raw[e][:], in_=w2[e].rearrange("(p j) c -> p j c", j=PACK))
 
         def load_w1(e):
             w1_raw[e] = raw.tile([P, PACK, K], F32, name="w1_raw", bufs=6)
@@ -92,25 +89,22 @@ def tile_moe_bdx_mlp_relu_kernel(tc, dyT, a, w2, w1, gate, offs, pos1, pos2, out
             quantize(g_q[q], 0, PAIR, g_bf[:])
 
         def make_w2(e):
-            w2_bf = mid.tile([P, H * PACK], BF16, name="w2_bf", bufs=3, align_bytes=64)
+            w2_bf = mid.tile([P, H * PACK], BF16, name="w2_bf", bufs=4, align_bytes=64)
             dst = w2_bf[:].rearrange("p (t m j) -> p m j t", t=PACK, j=PACK)
-            for i in range(2):
-                nc.scalar.copy(
-                    dst[:, i * 64 : (i + 1) * 64],
-                    w2_raw[e][i][:].rearrange("p j (m t) -> p m j t", t=PACK),
-                )
+            src = w2_raw[e][:].rearrange("p j (m t) -> p m j t", t=PACK)
+            nc.scalar.copy(dst, src)
             w2_q[e] = (
-                mid.tile([P, H], U32, name="w2_codes", bufs=5, align_bytes=64),
-                mid.tile([P, H], U8, name="w2_scales", bufs=5, align_bytes=64),
+                mid.tile([P, H], U32, name="w2_codes", bufs=4, align_bytes=64),
+                mid.tile([P, H], U8, name="w2_scales", bufs=4, align_bytes=64),
             )
             quantize(w2_q[e], 0, H, w2_bf[:])
 
         def cast_w1(e, h0, h1):
             if e not in w1_bf:
-                w1_bf[e] = mid.tile([P, K * PACK], BF16, name="w1_bf", bufs=5, align_bytes=64)
+                w1_bf[e] = mid.tile([P, K * PACK], BF16, name="w1_bf", bufs=6, align_bytes=64)
                 w1_q[e] = (
-                    mid.tile([P, K], U32, name="w1_codes", bufs=6, align_bytes=64),
-                    mid.tile([P, K], U8, name="w1_scales", bufs=6, align_bytes=64),
+                    mid.tile([P, K], U32, name="w1_codes", bufs=7, align_bytes=64),
+                    mid.tile([P, K], U8, name="w1_scales", bufs=7, align_bytes=64),
                 )
             lo, hi = h0 * 128, h1 * 128
             nc.scalar.copy(
@@ -147,8 +141,8 @@ def tile_moe_bdx_mlp_relu_kernel(tc, dyT, a, w2, w1, gate, offs, pos1, pos2, out
                     op1=ALU.mult,
                 )
             da_q[e] = (
-                mid.tile([P, C], U32, name="da_codes", bufs=6, align_bytes=64),
-                mid.tile([P, C], U8, name="da_scales", bufs=6, align_bytes=64),
+                mid.tile([P, C], U32, name="da_codes", bufs=7, align_bytes=64),
+                mid.tile([P, C], U8, name="da_scales", bufs=7, align_bytes=64),
             )
             quantize(da_q[e], 0, C, da_bf[:])
 
@@ -169,72 +163,82 @@ def tile_moe_bdx_mlp_relu_kernel(tc, dyT, a, w2, w1, gate, offs, pos1, pos2, out
 
         picked = {}
 
+        def half(h, which):
+            return picked[h][:].rearrange("p t m -> p (t m)")[:, which * T : (which + 1) * T]
+
         def pick(h, which, lo, hi):
-            if (h, which) not in picked:
-                picked[h, which] = mid.tile([P, T], F32, name=f"pick{which}", bufs=2)
+            if h not in picked:
+                picked[h] = mid.tile([P, PACK, PAIR], F32, name="g4", bufs=4)
             pos = (pos1_sb, pos2_sb)[which]
-            nc.vector.tensor_copy(picked[h, which][:, lo:hi], dx[h][:].indirect(pos[:, lo // 16 : hi // 16]))
+            nc.vector.tensor_copy(half(h, which)[:, lo:hi], dx[h][:].indirect(pos[:, lo // 16 : hi // 16]))
 
         def combine(h, lo, hi, engine):
-            o = picked[h, 0][:, lo:hi]
-            engine.tensor_tensor(o, o, picked[h, 1][:, lo:hi], ALU.add)
+            o = half(h, 0)[:, lo:hi]
+            engine.tensor_tensor(o, o, half(h, 1)[:, lo:hi], ALU.add)
             nc.sync.dma_start(out=out[h * P : (h + 1) * P, lo:hi], in_=o)
 
         nc.sync.dma_start(offs_sb[:], offs)
         load_dy(0)
         load_gate(0)
-        load_w2(0, (0,))
         load_gate(1)
-        load_w2(0, (1,))
-        load_gate(2)
-        load_w2(1, (0,))
-        load_gate(3)
-        load_w2(1, (1,))
         load_dy(1)
-        load_w2(2)
+        load_w2(0)
         load_dy(2)
-        load_w2(3, (0,))
         load_dy(3)
-        load_w1(0)
-        load_w2(3, (1,))
+        load_w2(1)
+        load_gate(2)
         load_a(0)
+        load_w2(2)
+        load_gate(3)
+        load_w2(3)
+        load_w1(0)
         load_w1(1)
-        nc.sync.dma_start(pos1_sb[:], pos1)
-        nc.sync.dma_start(pos2_sb[:], pos2)
-
-        make_w2(0)
-        make_w2(1)
-        make_w2(2)
-        gather(0)
-        gather(1)
-        make_g(0)
-        make_w2(3)
         load_a(1)
         load_w1(2)
         load_w1(3)
+        nc.sync.dma_start(pos1_sb[:], pos1)
+        nc.sync.dma_start(pos2_sb[:], pos2)
+
         for q in range(PAIRS):
-            for e in (2 * q, 2 * q + 1):
-                if e + 4 < E:
-                    load_w2(e + 4)
-            if q + 2 < PAIRS:
-                load_w1(2 * q + 4)
-                load_a(q + 2)
-                load_w1(2 * q + 5)
-            for e in (2 * q, 2 * q + 1):
-                stage1(e)
-            if q + 2 < PAIRS:
-                gather(q + 2)
-            if q + 1 < PAIRS:
-                make_g(q + 1)
-            for e in (2 * q, 2 * q + 1):
-                hh = 2 if e < EARLY else 1
-                cast_w1(e, 0, hh)
-                quantize_w1(e, 0, hh)
-                if e + 4 < E:
-                    make_w2(e + 4)
+            gather(q)
+        make_w2(0)
+        make_g(0)
+        make_w2(1)
+        make_g(1)
+        make_w2(2)
+        make_w2(3)
+        load_w2(4)
+        load_w2(5)
+        load_a(2)
+        load_w2(6)
+        load_w2(7)
+        load_a(3)
+        for e in range(4, E):
+            load_w1(e)
+        for e in range(4):
+            stage1(e)
+        for e in range(4):
+            cast_w1(e, 0, 2 if e < EARLY else 1)
+            quantize_w1(e, 0, 2 if e < EARLY else 1)
+        make_g(2)
+        make_w2(4)
+        make_w2(5)
+        stage2(0, 0)
+        stage2(1, 0)
+        for q in range(EARLY // 2):
+            stage2(q, 1)
+        make_g(3)
+        stage1(4)
+        stage1(5)
+        make_w2(6)
+        make_w2(7)
+        stage1(6)
+        stage1(7)
+        for e in range(4, E):
+            cast_w1(e, 0, 1)
+            quantize_w1(e, 0, 1)
+        for q in range(2, PAIRS):
             stage2(q, 0)
-            if 2 * q < EARLY:
-                stage2(q, 1)
         for e in range(EARLY, E):
             cast_w1(e, 1, 2)
         pick(0, 0, 0, T)

@@ -20,7 +20,142 @@ PACK = 4
 PAIR = 2 * C
 PAIRS = E // 2
 CHUNK = 128
-EARLY = 2
+PLAN = [
+    ("off", ()),
+    ("dy", (0,)),
+    ("gate", (0,)),
+    ("dy", (1,)),
+    ("ga", (0, 0,)),
+    ("dy", (2,)),
+    ("gate", (1,)),
+    ("lw2", (0,)),
+    ("lw2", (1,)),
+    ("gate", (2,)),
+    ("lw2", (2,)),
+    ("gate", (3,)),
+    ("ga", (1, 0,)),
+    ("lw2", (3,)),
+    ("lw2", (4,)),
+    ("cw2", (0,)),
+    ("qw2", (0,)),
+    ("ga", (0, 1,)),
+    ("lw2", (5,)),
+    ("dy", (3,)),
+    ("lw1", (0,)),
+    ("lw1", (1,)),
+    ("cw2", (1,)),
+    ("qw2", (1,)),
+    ("ga", (1, 1,)),
+    ("ga", (0, 3,)),
+    ("ga", (2, 0,)),
+    ("lw1", (2,)),
+    ("ga", (0, 2,)),
+    ("ga", (1, 2,)),
+    ("lw1", (3,)),
+    ("ga", (3, 0,)),
+    ("cw1", (0, 0, 1, "V",)),
+    ("qw1", (0, 0, 1,)),
+    ("cw1", (0, 1, 2, "S",)),
+    ("qw1", (0, 1, 2,)),
+    ("la", (0,)),
+    ("lw1", (4,)),
+    ("la", (1,)),
+    ("lw1", (5,)),
+    ("lw2", (6,)),
+    ("ga", (1, 3,)),
+    ("lw2", (7,)),
+    ("cw1", (1, 0, 2, "V",)),
+    ("qw1", (1, 0, 2,)),
+    ("ga", (2, 2,)),
+    ("cg", (0,)),
+    ("qg", (0,)),
+    ("ga", (2, 3,)),
+    ("la", (2,)),
+    ("s1", (0, 0,)),
+    ("s1", (0, 1,)),
+    ("qda", (0,)),
+    ("cw2", (2,)),
+    ("qw2", (2,)),
+    ("cg", (1,)),
+    ("qg", (1,)),
+    ("ga", (2, 1,)),
+    ("s1", (1, 0,)),
+    ("s1", (1, 1,)),
+    ("qda", (1,)),
+    ("cw1", (2, 0, 2, "V",)),
+    ("qw1", (2, 0, 2,)),
+    ("s1", (2, 0,)),
+    ("s1", (2, 1,)),
+    ("qda", (2,)),
+    ("pos", ()),
+    ("cw2", (3,)),
+    ("qw2", (3,)),
+    ("la", (3,)),
+    ("cg", (2,)),
+    ("qg", (2,)),
+    ("cw1", (3, 0, 2, "S",)),
+    ("qw1", (3, 0, 2,)),
+    ("s2", (0, 0,)),
+    ("s2", (0, 1,)),
+    ("cw2", (4,)),
+    ("qw2", (4,)),
+    ("s1", (3, 0,)),
+    ("s1", (3, 1,)),
+    ("qda", (3,)),
+    ("s1", (4, 0,)),
+    ("s1", (4, 1,)),
+    ("qda", (4,)),
+    ("lw1", (6,)),
+    ("lw1", (7,)),
+    ("cw1", (4, 0, 2, "V",)),
+    ("qw1", (4, 0, 2,)),
+    ("ga", (3, 1,)),
+    ("cw1", (5, 0, 1, "S",)),
+    ("qw1", (5, 0, 1,)),
+    ("cw1", (5, 1, 2, "V",)),
+    ("qw1", (5, 1, 2,)),
+    ("ga", (3, 3,)),
+    ("ga", (3, 2,)),
+    ("cg", (3,)),
+    ("qg", (3,)),
+    ("cw2", (5,)),
+    ("qw2", (5,)),
+    ("s2", (1, 0,)),
+    ("s2", (1, 1,)),
+    ("s1", (5, 0,)),
+    ("s1", (5, 1,)),
+    ("qda", (5,)),
+    ("cw1", (6, 0, 2, "S",)),
+    ("qw1", (6, 0, 2,)),
+    ("cw1", (7, 0, 2, "S",)),
+    ("qw1", (7, 0, 2,)),
+    ("cw2", (6,)),
+    ("qw2", (6,)),
+    ("s2", (2, 0,)),
+    ("s2", (2, 1,)),
+    ("s1", (6, 0,)),
+    ("s1", (6, 1,)),
+    ("qda", (6,)),
+    ("cw2", (7,)),
+    ("qw2", (7,)),
+    ("s1", (7, 0,)),
+    ("s1", (7, 1,)),
+    ("qda", (7,)),
+    ("s2", (3, 0,)),
+    ("s2", (3, 1,)),
+    ("pk", (0, 0, 0, 1024,)),
+    ("pk", (0, 1, 0, 512,)),
+    ("cb", (0, 0, 512, "G",)),
+    ("pk", (0, 1, 512, 1024,)),
+    ("cb", (0, 512, 1024, "G",)),
+    ("pk", (1, 0, 0, 1024,)),
+    ("pk", (1, 1, 0, 512,)),
+    ("cb", (1, 0, 512, "G",)),
+    ("pk", (1, 1, 512, 768,)),
+    ("pk", (1, 1, 768, 1024,)),
+    ("cb", (1, 512, 768, "V",)),
+    ("cb", (1, 768, 1024, "V",)),
+]
 
 
 def tile_moe_bdx_mlp_relu_kernel(tc, dyT, a, w2, w1, gate, offs, pos1, pos2, out):
@@ -61,11 +196,13 @@ def tile_moe_bdx_mlp_relu_kernel(tc, dyT, a, w2, w1, gate, offs, pos1, pos2, out
             a_raw[q] = raw.tile([P, PACK, PAIR], F32, name="a_raw", bufs=3)
             nc.sync.dma_start(out=a_raw[q][:], in_=a_view[:, :, q * PAIR : (q + 1) * PAIR])
 
+        w2_bfs, g_bfs, da_bfs = {}, {}, {}
         w2_q, w1_bf, w1_q, g_q, da_q, g4 = {}, {}, {}, {}, {}, {}
 
-        def gather(q):
-            g4[q] = mid.tile([P, PACK, PAIR], F32, name="g4", bufs=4)
-            for t in range(PACK):
+        def gather(q, t0):
+            if q not in g4:
+                g4[q] = mid.tile([P, PACK, PAIR], F32, name="g4", bufs=4)
+            for t in (t0,):
                 nc.vector.tensor_tensor(
                     g4[q][:, t, :],
                     dy[t][:].indirect(offs_sb[:, q * (PAIR // 16) : (q + 1) * (PAIR // 16)]),
@@ -78,6 +215,7 @@ def tile_moe_bdx_mlp_relu_kernel(tc, dyT, a, w2, w1, gate, offs, pos1, pos2, out
 
         def make_g(q):
             g_bf = mid.tile([P, PAIR * PACK], BF16, name="g_bf", bufs=2, align_bytes=64)
+            g_bfs[q] = g_bf
             nc.scalar.copy(
                 g_bf[:].rearrange("p (c i t) -> p c t i", i=4, t=PACK),
                 g4[q][:].rearrange("p t (c i) -> p c t i", i=4),
@@ -86,20 +224,25 @@ def tile_moe_bdx_mlp_relu_kernel(tc, dyT, a, w2, w1, gate, offs, pos1, pos2, out
                 mid.tile([P, PAIR], U32, name="g_codes", bufs=2, align_bytes=64),
                 mid.tile([P, PAIR], U8, name="g_scales", bufs=2, align_bytes=64),
             )
-            quantize(g_q[q], 0, PAIR, g_bf[:])
+
+        def quant_g(q):
+            quantize(g_q[q], 0, PAIR, g_bfs[q][:])
 
         def make_w2(e):
             w2_bf = mid.tile([P, H * PACK], BF16, name="w2_bf", bufs=4, align_bytes=64)
             dst = w2_bf[:].rearrange("p (t m j) -> p m j t", t=PACK, j=PACK)
             src = w2_raw[e][:].rearrange("p j (m t) -> p m j t", t=PACK)
+            w2_bfs[e] = w2_bf
             nc.scalar.copy(dst, src)
             w2_q[e] = (
                 mid.tile([P, H], U32, name="w2_codes", bufs=4, align_bytes=64),
                 mid.tile([P, H], U8, name="w2_scales", bufs=4, align_bytes=64),
             )
-            quantize(w2_q[e], 0, H, w2_bf[:])
 
-        def cast_w1(e, h0, h1):
+        def quant_w2(e):
+            quantize(w2_q[e], 0, H, w2_bfs[e][:])
+
+        def cast_w1(e, h0, h1, eng="S"):
             if e not in w1_bf:
                 w1_bf[e] = mid.tile([P, K * PACK], BF16, name="w1_bf", bufs=6, align_bytes=64)
                 w1_q[e] = (
@@ -107,7 +250,7 @@ def tile_moe_bdx_mlp_relu_kernel(tc, dyT, a, w2, w1, gate, offs, pos1, pos2, out
                     mid.tile([P, K], U8, name="w1_scales", bufs=7, align_bytes=64),
                 )
             lo, hi = h0 * 128, h1 * 128
-            nc.scalar.copy(
+            (nc.scalar.copy if eng == "S" else nc.vector.tensor_copy if eng == "V" else nc.gpsimd.tensor_copy)(
                 w1_bf[e][:, lo * PACK : hi * PACK].rearrange("p (c i t) -> p c t i", i=4, t=PACK),
                 w1_raw[e][:, :, lo:hi].rearrange("p t (c i) -> p c t i", i=4),
             )
@@ -116,10 +259,12 @@ def tile_moe_bdx_mlp_relu_kernel(tc, dyT, a, w2, w1, gate, offs, pos1, pos2, out
             lo, hi = h0 * 128, h1 * 128
             quantize(w1_q[e], lo, hi, w1_bf[e][:, lo * PACK : hi * PACK])
 
-        def stage1(e):
+        def stage1(e, c0):
             q, base = e // 2, (e % 2) * C
-            da_bf = mid.tile([P, C * PACK], BF16, name="da_bf", bufs=3, align_bytes=64)
-            for c in range(C // CHUNK):
+            if e not in da_bfs:
+                da_bfs[e] = mid.tile([P, C * PACK], BF16, name="da_bf", bufs=3, align_bytes=64)
+            da_bf = da_bfs[e]
+            for c in (c0,):
                 lo = base + c * CHUNK
                 bank = psum.tile([P, PACK, CHUNK], F32, name="bank1", bufs=5)
                 for t in range(PACK):
@@ -140,6 +285,9 @@ def tile_moe_bdx_mlp_relu_kernel(tc, dyT, a, w2, w1, gate, offs, pos1, pos2, out
                     op0=ALU.is_gt,
                     op1=ALU.mult,
                 )
+
+        def quant_da(e):
+            da_bf = da_bfs[e]
             da_q[e] = (
                 mid.tile([P, C], U32, name="da_codes", bufs=7, align_bytes=64),
                 mid.tile([P, C], U8, name="da_scales", bufs=7, align_bytes=64),
@@ -177,83 +325,14 @@ def tile_moe_bdx_mlp_relu_kernel(tc, dyT, a, w2, w1, gate, offs, pos1, pos2, out
             engine.tensor_tensor(o, o, half(h, 1)[:, lo:hi], ALU.add)
             nc.sync.dma_start(out=out[h * P : (h + 1) * P, lo:hi], in_=o)
 
-        nc.sync.dma_start(offs_sb[:], offs)
-        load_dy(0)
-        load_gate(0)
-        load_gate(1)
-        load_dy(1)
-        load_w2(0)
-        load_dy(2)
-        load_dy(3)
-        load_w2(1)
-        load_gate(2)
-        load_a(0)
-        load_w2(2)
-        load_gate(3)
-        load_w2(3)
-        load_w1(0)
-        load_w1(1)
-        load_a(1)
-        load_w1(2)
-        load_w1(3)
-        nc.sync.dma_start(pos1_sb[:], pos1)
-        nc.sync.dma_start(pos2_sb[:], pos2)
 
-        for q in range(PAIRS):
-            gather(q)
-        make_w2(0)
-        make_g(0)
-        make_w2(1)
-        make_g(1)
-        make_w2(2)
-        make_w2(3)
-        load_w2(4)
-        load_w2(5)
-        load_a(2)
-        load_w2(6)
-        load_w2(7)
-        load_a(3)
-        for e in range(4, E):
-            load_w1(e)
-        for e in range(4):
-            stage1(e)
-        for e in range(4):
-            cast_w1(e, 0, 2 if e < EARLY else 1)
-            quantize_w1(e, 0, 2 if e < EARLY else 1)
-        make_g(2)
-        make_w2(4)
-        make_w2(5)
-        stage2(0, 0)
-        stage2(1, 0)
-        for q in range(EARLY // 2):
-            stage2(q, 1)
-        make_g(3)
-        stage1(4)
-        stage1(5)
-        make_w2(6)
-        make_w2(7)
-        stage1(6)
-        stage1(7)
-        for e in range(4, E):
-            cast_w1(e, 0, 1)
-            quantize_w1(e, 0, 1)
-        for q in range(2, PAIRS):
-            stage2(q, 0)
-        for e in range(EARLY, E):
-            cast_w1(e, 1, 2)
-        pick(0, 0, 0, T)
-        for e in range(EARLY, E):
-            quantize_w1(e, 1, 2)
-        for q in range(EARLY // 2, PAIRS):
-            stage2(q, 1)
-        pick(0, 1, 0, T // 2)
-        combine(0, 0, T // 2, nc.gpsimd)
-        pick(0, 1, T // 2, T)
-        combine(0, T // 2, T, nc.gpsimd)
-        pick(1, 0, 0, T)
-        pick(1, 1, 0, T // 2)
-        combine(1, 0, T // 2, nc.gpsimd)
-        pick(1, 1, T // 2, 3 * T // 4)
-        pick(1, 1, 3 * T // 4, T)
-        combine(1, T // 2, 3 * T // 4, nc.vector)
-        combine(1, 3 * T // 4, T, nc.vector)
+        def load_off():
+            nc.sync.dma_start(offs_sb[:], offs)
+
+        def load_pos():
+            nc.sync.dma_start(pos1_sb[:], pos1)
+            nc.sync.dma_start(pos2_sb[:], pos2)
+
+        FN = dict(off=load_off, pos=load_pos, dy=load_dy, gate=load_gate, lw2=load_w2, lw1=load_w1, la=load_a, ga=gather, cg=make_g, qg=quant_g, cw2=make_w2, qw2=quant_w2, cw1=cast_w1, qw1=quantize_w1, s1=stage1, qda=quant_da, s2=stage2, pk=pick, cb=lambda h, lo, hi, e: combine(h, lo, hi, nc.gpsimd if e == "G" else nc.vector))
+        for f, args in PLAN:
+            FN[f](*args)

from contextlib import ExitStack

import concourse.mybir as mybir

K, T, E, C, H, N = 256, 1024, 8, 256, 512, 512
S = E * C
FLOPS = 2 * S * N * H + 2 * S * H * K
BYTES = 4 * (N * T + H * S + E * N * H + E * H * K + S + K * T) + 2 * 128 * (S + 2 * T) // 16

F32 = mybir.dt.float32
BF16 = mybir.dt.bfloat16
U32 = mybir.dt.uint32
U16 = mybir.dt.uint16
U8 = mybir.dt.uint8
FP8X4 = mybir.dt.float8_e4m3fn_x4
ALU = mybir.AluOpType

P = 128
PACK = 4
PAIR = 2 * C
PAIRS = E // 2
CHUNK = 128
PLAN = [
    ("off", ()),
    ("dy", (0,)),
    ("gate", (0,)),
    ("dy", (1,)),
    ("ga", (0, 0,)),
    ("dy", (2,)),
    ("gate", (1,)),
    ("lw2", (0,)),
    ("lw2", (1,)),
    ("gate", (2,)),
    ("lw2", (2,)),
    ("gate", (3,)),
    ("ga", (1, 0,)),
    ("lw2", (3,)),
    ("lw2", (4,)),
    ("cw2", (0,)),
    ("qw2", (0,)),
    ("ga", (0, 1,)),
    ("lw2", (5,)),
    ("dy", (3,)),
    ("lw1", (0,)),
    ("lw1", (1,)),
    ("cw2", (1,)),
    ("qw2", (1,)),
    ("ga", (1, 1,)),
    ("ga", (0, 3,)),
    ("ga", (2, 0,)),
    ("lw1", (2,)),
    ("ga", (0, 2,)),
    ("ga", (1, 2,)),
    ("lw1", (3,)),
    ("ga", (3, 0,)),
    ("cw1", (0, 0, 1, "V",)),
    ("qw1", (0, 0, 1,)),
    ("cw1", (0, 1, 2, "S",)),
    ("qw1", (0, 1, 2,)),
    ("la", (0,)),
    ("lw1", (4,)),
    ("la", (1,)),
    ("lw1", (5,)),
    ("lw2", (6,)),
    ("ga", (1, 3,)),
    ("lw2", (7,)),
    ("cw1", (1, 0, 2, "V",)),
    ("qw1", (1, 0, 2,)),
    ("ga", (2, 2,)),
    ("cg", (0,)),
    ("qg", (0,)),
    ("ga", (2, 3,)),
    ("la", (2,)),
    ("s1", (0, 0,)),
    ("s1", (0, 1,)),
    ("qda", (0,)),
    ("cw2", (2,)),
    ("qw2", (2,)),
    ("cg", (1,)),
    ("qg", (1,)),
    ("ga", (2, 1,)),
    ("s1", (1, 0,)),
    ("s1", (1, 1,)),
    ("qda", (1,)),
    ("cw1", (2, 0, 2, "V",)),
    ("qw1", (2, 0, 2,)),
    ("s1", (2, 0,)),
    ("s1", (2, 1,)),
    ("qda", (2,)),
    ("pos", ()),
    ("cw2", (3,)),
    ("qw2", (3,)),
    ("la", (3,)),
    ("cg", (2,)),
    ("qg", (2,)),
    ("cw1", (3, 0, 2, "S",)),
    ("qw1", (3, 0, 2,)),
    ("s2", (0, 0,)),
    ("s2", (0, 1,)),
    ("cw2", (4,)),
    ("qw2", (4,)),
    ("s1", (3, 0,)),
    ("s1", (3, 1,)),
    ("qda", (3,)),
    ("s1", (4, 0,)),
    ("s1", (4, 1,)),
    ("qda", (4,)),
    ("lw1", (6,)),
    ("lw1", (7,)),
    ("cw1", (4, 0, 2, "V",)),
    ("qw1", (4, 0, 2,)),
    ("ga", (3, 1,)),
    ("cw1", (5, 0, 1, "S",)),
    ("qw1", (5, 0, 1,)),
    ("cw1", (5, 1, 2, "V",)),
    ("qw1", (5, 1, 2,)),
    ("ga", (3, 3,)),
    ("ga", (3, 2,)),
    ("cg", (3,)),
    ("qg", (3,)),
    ("cw2", (5,)),
    ("qw2", (5,)),
    ("s2", (1, 0,)),
    ("s2", (1, 1,)),
    ("s1", (5, 0,)),
    ("s1", (5, 1,)),
    ("qda", (5,)),
    ("cw1", (6, 0, 2, "S",)),
    ("qw1", (6, 0, 2,)),
    ("cw1", (7, 0, 2, "S",)),
    ("qw1", (7, 0, 2,)),
    ("cw2", (6,)),
    ("qw2", (6,)),
    ("s2", (2, 0,)),
    ("s2", (2, 1,)),
    ("s1", (6, 0,)),
    ("s1", (6, 1,)),
    ("qda", (6,)),
    ("cw2", (7,)),
    ("qw2", (7,)),
    ("s1", (7, 0,)),
    ("s1", (7, 1,)),
    ("qda", (7,)),
    ("s2", (3, 0,)),
    ("s2", (3, 1,)),
    ("pk", (0, 0, 0, 1024,)),
    ("pk", (0, 1, 0, 512,)),
    ("cb", (0, 0, 512, "G",)),
    ("pk", (0, 1, 512, 1024,)),
    ("cb", (0, 512, 1024, "G",)),
    ("pk", (1, 0, 0, 1024,)),
    ("pk", (1, 1, 0, 512,)),
    ("cb", (1, 0, 512, "G",)),
    ("pk", (1, 1, 512, 768,)),
    ("pk", (1, 1, 768, 1024,)),
    ("cb", (1, 512, 768, "V",)),
    ("cb", (1, 768, 1024, "V",)),
]


def tile_moe_bdx_mlp_relu_kernel(tc, dyT, a, w2, w1, gate, offs, pos1, pos2, out):
    nc = tc.nc
    with ExitStack() as ctx:
        held = ctx.enter_context(tc.tile_pool(name="held", bufs=1))
        raw = ctx.enter_context(tc.tile_pool(name="raw", bufs=4))
        mid = ctx.enter_context(tc.tile_pool(name="mid", bufs=3))
        psum = ctx.enter_context(tc.psum_pool(name="psum", bufs=5))

        offs_sb = held.tile([P, S // 16], U16, name="offs_sb")
        pos1_sb = held.tile([P, T // 16], U16, name="pos1_sb")
        pos2_sb = held.tile([P, T // 16], U16, name="pos2_sb")
        dy = [held.tile([P, T], F32, name=f"dy{t}") for t in range(PACK)]
        gates = [held.tile([P, PAIR], F32, name=f"gate{q}") for q in range(PAIRS)]
        dx = [held.tile([P, S], F32, name=f"dx{h}") for h in range(2)]

        dy_view = dyT.rearrange("(p t) m -> p t m", t=PACK)
        a_view = a.rearrange("(p t) m -> p t m", t=PACK)

        w2_raw, w1_raw, a_raw = {}, {}, {}

        def load_dy(t):
            nc.sync.dma_start(out=dy[t][:], in_=dy_view[:, t, :])

        def load_gate(q):
            nc.sync.dma_start(out=gates[q][:], in_=gate[0:P, q * PAIR : (q + 1) * PAIR])

        def load_w2(e):
            w2_raw[e] = raw.tile([P, PACK, H], F32, name="w2_raw", bufs=4)
            nc.sync.dma_start(out=w2_raw[e][:], in_=w2[e].rearrange("(p j) c -> p j c", j=PACK))

        def load_w1(e):
            w1_raw[e] = raw.tile([P, PACK, K], F32, name="w1_raw", bufs=6)
            nc.sync.dma_start(out=w1_raw[e][:], in_=w1[e].rearrange("(p j) c -> p j c", j=PACK))

        def load_a(q):
            a_raw[q] = raw.tile([P, PACK, PAIR], F32, name="a_raw", bufs=3)
            nc.sync.dma_start(out=a_raw[q][:], in_=a_view[:, :, q * PAIR : (q + 1) * PAIR])

        w2_bfs, g_bfs, da_bfs = {}, {}, {}
        w2_q, w1_bf, w1_q, g_q, da_q, g4 = {}, {}, {}, {}, {}, {}

        def gather(q, t0):
            if q not in g4:
                g4[q] = mid.tile([P, PACK, PAIR], F32, name="g4", bufs=4)
            for t in (t0,):
                nc.vector.tensor_tensor(
                    g4[q][:, t, :],
                    dy[t][:].indirect(offs_sb[:, q * (PAIR // 16) : (q + 1) * (PAIR // 16)]),
                    gates[q][:],
                    ALU.mult,
                )

        def quantize(dst, lo, hi, src):
            nc.vector.quantize_mx(out=dst[0][:, lo:hi].bitcast(FP8X4), scales=dst[1][:, lo:hi], in_=src)

        def make_g(q):
            g_bf = mid.tile([P, PAIR * PACK], BF16, name="g_bf", bufs=2, align_bytes=64)
            g_bfs[q] = g_bf
            nc.scalar.copy(
                g_bf[:].rearrange("p (c i t) -> p c t i", i=4, t=PACK),
                g4[q][:].rearrange("p t (c i) -> p c t i", i=4),
            )
            g_q[q] = (
                mid.tile([P, PAIR], U32, name="g_codes", bufs=2, align_bytes=64),
                mid.tile([P, PAIR], U8, name="g_scales", bufs=2, align_bytes=64),
            )

        def quant_g(q):
            quantize(g_q[q], 0, PAIR, g_bfs[q][:])

        def make_w2(e):
            w2_bf = mid.tile([P, H * PACK], BF16, name="w2_bf", bufs=4, align_bytes=64)
            dst = w2_bf[:].rearrange("p (t m j) -> p m j t", t=PACK, j=PACK)
            src = w2_raw[e][:].rearrange("p j (m t) -> p m j t", t=PACK)
            w2_bfs[e] = w2_bf
            nc.scalar.copy(dst, src)
            w2_q[e] = (
                mid.tile([P, H], U32, name="w2_codes", bufs=4, align_bytes=64),
                mid.tile([P, H], U8, name="w2_scales", bufs=4, align_bytes=64),
            )

        def quant_w2(e):
            quantize(w2_q[e], 0, H, w2_bfs[e][:])

        def cast_w1(e, h0, h1, eng="S"):
            if e not in w1_bf:
                w1_bf[e] = mid.tile([P, K * PACK], BF16, name="w1_bf", bufs=6, align_bytes=64)
                w1_q[e] = (
                    mid.tile([P, K], U32, name="w1_codes", bufs=7, align_bytes=64),
                    mid.tile([P, K], U8, name="w1_scales", bufs=7, align_bytes=64),
                )
            lo, hi = h0 * 128, h1 * 128
            (nc.scalar.copy if eng == "S" else nc.vector.tensor_copy if eng == "V" else nc.gpsimd.tensor_copy)(
                w1_bf[e][:, lo * PACK : hi * PACK].rearrange("p (c i t) -> p c t i", i=4, t=PACK),
                w1_raw[e][:, :, lo:hi].rearrange("p t (c i) -> p c t i", i=4),
            )

        def quantize_w1(e, h0, h1):
            lo, hi = h0 * 128, h1 * 128
            quantize(w1_q[e], lo, hi, w1_bf[e][:, lo * PACK : hi * PACK])

        def stage1(e, c0):
            q, base = e // 2, (e % 2) * C
            if e not in da_bfs:
                da_bfs[e] = mid.tile([P, C * PACK], BF16, name="da_bf", bufs=3, align_bytes=64)
            da_bf = da_bfs[e]
            for c in (c0,):
                lo = base + c * CHUNK
                bank = psum.tile([P, PACK, CHUNK], F32, name="bank1", bufs=5)
                for t in range(PACK):
                    nc.tensor.matmul_mx(
                        out=bank[:, t, :],
                        lhsT=w2_q[e][0][:, t * P : (t + 1) * P].bitcast(FP8X4),
                        lhsT_scale=w2_q[e][1][:, t * P : (t + 1) * P],
                        rhs=g_q[q][0][:, lo : lo + CHUNK].bitcast(FP8X4),
                        rhs_scale=g_q[q][1][:, lo : lo + CHUNK],
                        start=True,
                        stop=True,
                    )
                nc.vector.scalar_tensor_tensor(
                    out=da_bf[:, c * CHUNK * PACK : (c + 1) * CHUNK * PACK].rearrange("p (m t) -> p m t", t=PACK),
                    in0=a_raw[q][:, :, lo : lo + CHUNK].rearrange("p t m -> p m t"),
                    scalar=0.0,
                    in1=bank[:].rearrange("p t m -> p m t"),
                    op0=ALU.is_gt,
                    op1=ALU.mult,
                )

        def quant_da(e):
            da_bf = da_bfs[e]
            da_q[e] = (
                mid.tile([P, C], U32, name="da_codes", bufs=7, align_bytes=64),
                mid.tile([P, C], U8, name="da_scales", bufs=7, align_bytes=64),
            )
            quantize(da_q[e], 0, C, da_bf[:])

        def stage2(q, h):
            bank = psum.tile([P, PAIR], F32, name="bank2", bufs=3)
            for i in range(2):
                e = 2 * q + i
                nc.tensor.matmul_mx(
                    out=bank[:, i * C : (i + 1) * C],
                    lhsT=w1_q[e][0][:, h * P : (h + 1) * P].bitcast(FP8X4),
                    lhsT_scale=w1_q[e][1][:, h * P : (h + 1) * P],
                    rhs=da_q[e][0][:].bitcast(FP8X4),
                    rhs_scale=da_q[e][1][:],
                    start=True,
                    stop=True,
                )
            nc.scalar.copy(dx[h][:, q * PAIR : (q + 1) * PAIR], bank[:])

        picked = {}

        def half(h, which):
            return picked[h][:].rearrange("p t m -> p (t m)")[:, which * T : (which + 1) * T]

        def pick(h, which, lo, hi):
            if h not in picked:
                picked[h] = mid.tile([P, PACK, PAIR], F32, name="g4", bufs=4)
            pos = (pos1_sb, pos2_sb)[which]
            nc.vector.tensor_copy(half(h, which)[:, lo:hi], dx[h][:].indirect(pos[:, lo // 16 : hi // 16]))

        def combine(h, lo, hi, engine):
            o = half(h, 0)[:, lo:hi]
            engine.tensor_tensor(o, o, half(h, 1)[:, lo:hi], ALU.add)
            nc.sync.dma_start(out=out[h * P : (h + 1) * P, lo:hi], in_=o)


        def load_off():
            nc.sync.dma_start(offs_sb[:], offs)

        def load_pos():
            nc.sync.dma_start(pos1_sb[:], pos1)
            nc.sync.dma_start(pos2_sb[:], pos2)

        FN = dict(off=load_off, pos=load_pos, dy=load_dy, gate=load_gate, lw2=load_w2, lw1=load_w1, la=load_a, ga=gather, cg=make_g, qg=quant_g, cw2=make_w2, qw2=quant_w2, cw1=cast_w1, qw1=quantize_w1, s1=stage1, qda=quant_da, s2=stage2, pk=pick, cb=lambda h, lo, hi, e: combine(h, lo, hi, nc.gpsimd if e == "G" else nc.vector))
        for f, args in PLAN:
            FN[f](*args)
